import numpy as np
import ml_dtypes


def mxq(x, axis, fmt="e4m3"):
    dtype, down = {"e4m3": (ml_dtypes.float8_e4m3fn, 7), "e5m2": (ml_dtypes.float8_e5m2, 14)}[fmt]
    v = np.moveaxis(np.asarray(x, np.float32).astype(ml_dtypes.bfloat16).astype(np.float64), axis, -1)
    blocks = v.reshape(v.shape[:-1] + (-1, 32))
    amax = np.abs(blocks).max(-1, keepdims=True)
    byte = np.maximum(np.where(amax > 0, np.frexp(amax)[1] - 1 + 127, 0) - down, 1)
    scale = np.exp2(byte - 127.0)
    codes = (blocks / scale).astype(np.float32).astype(dtype).astype(np.float64)
    return np.moveaxis((codes * scale).reshape(v.shape), -1, axis)


WIDE = False


def mx_kscale(k):
    if not WIDE:
        return np.ones(k)
    levels = np.array([10, -10, 5, -5, 0])
    if k % 512:
        return np.exp2(np.random.permutation(np.resize(levels, k // 32))).repeat(32)
    a = np.empty((k // 512, 16))
    for p in range(k // 512):
        a[p, :8] = np.random.permutation(np.resize(levels, 8))
        for g in range(8):
            far = levels[np.abs(levels - a[p, g]) >= 10]
            a[p, g + 8] = far[np.random.randint(len(far))]
    return np.exp2(a.ravel()).repeat(32)


def f64(x):
    return np.asarray(x).astype(np.float64)


def striped(idx):
    return np.tile(idx.reshape(-1, 16).T, (8, 1)).astype(np.uint16)


def unstriped(offs):
    return offs[:16].T.reshape(-1).astype(np.int64)


def pack_weight(w):
    k, n = w.shape
    w = f64(np.asarray(w, np.float32).astype(ml_dtypes.bfloat16)).reshape(k // 32, 32, n)
    amax = np.abs(w).max(1)
    byte = np.clip(np.where(amax > 0, np.frexp(amax)[1] - 1 + 127 - 7, 1), 1, 254)
    scaled = (w * np.exp2(127.0 - byte)[:, None, :]).reshape(k, n).astype(np.float32)
    words = np.ascontiguousarray(scaled.reshape(k // 512, 128, 4, n).transpose(0, 1, 3, 2)).astype(ml_dtypes.float8_e4m3fn).view(np.uint8)
    return words, np.ascontiguousarray(byte.astype(np.uint8).reshape(k // 512, 16, n))


def unpack_weight(words, scales):
    g, p, n, _ = words.shape
    vals = np.ascontiguousarray(words).view(ml_dtypes.float8_e4m3fn).astype(np.float64) * np.repeat(np.exp2(scales.astype(np.float64) - 127.0), 8, axis=1)[..., None]
    return vals.transpose(0, 1, 3, 2).reshape(g * 512, n)


def relu2(v):
    return np.maximum(v, 0.0) ** 2


K, T, S, N = 1024, 2048, 1024, 128


def setup_inputs():
    n = np.random.standard_normal
    s = mx_kscale(K)[:, None]
    words, scales = pack_weight(n((K, N)) / np.sqrt(K) / s)
    return {
        "xT": (n((K, T)) * s).astype(np.float32),
        "w_words": words,
        "w_scales": scales,
        "b": (0.3 * n((N, 1))).astype(np.float32),
        "offs": striped(np.random.permutation(T)[:S]),
    }


def reference(xT, w_words, w_scales, b, offs):
    w = unpack_weight(w_words, w_scales)
    idx = unstriped(offs)
    xq = mxq(f64(xT)[:, idx], 0, "e4m3")
    y = w.T @ xq
    y = relu2(y + f64(b))
    return y

@@ -1,0 +1,146 @@
+from contextlib import ExitStack
+
+import concourse.mybir as mybir
+
+K, T, S, M = 1024, 2048, 1024, 128
+P = 128
+FLOPS = 2 * K * S * M
+
+F32 = mybir.dt.float32
+BF16 = mybir.dt.bfloat16
+I32 = mybir.dt.int32
+U32 = mybir.dt.uint32
+U16 = mybir.dt.uint16
+U8 = mybir.dt.uint8
+FP8X4 = mybir.dt.float8_e4m3fn_x4
+ACT = mybir.ActivationFunctionType
+ALU = mybir.AluOpType
+
+PIECE = 256
+
+
+def tile_picked_pick_lin_relu2_sub_e_kernel(tc, xT, w_words, w_scales, b, offs, out):
+    nc = tc.nc
+    with ExitStack() as ctx:
+        keep = ctx.enter_context(tc.tile_pool(name="keep", bufs=1))
+        psum = ctx.enter_context(tc.psum_pool(name="psum", bufs=1))
+
+        quarters = [
+            (0, 0, [(1024, 640), (1024, 640)]),
+            (0, 1, [(1024, 256), (1024, 640)]),
+            (1, 0, [(1024, 0), (1024, 640)]),
+            (1, 1, [(768, 0), (768, 0), (512, 320)]),
+        ]
+
+        w_codes = keep.tile([P, 2, M], I32, align_bytes=64, name="w_codes")
+        w_bytes = keep.tile([P, 2, M], U8, align_bytes=64, name="w_bytes")
+        bias = keep.tile([P, 1], F32, name="bias")
+        nc.gpsimd.memset(w_bytes[:], 0)
+        offsets = keep.tile([P, S // 16], U16, name="offsets")
+        raws = {}
+        for i, (a, u, chunks) in enumerate(quarters):
+            src = xT[512 * a : 512 * (a + 1), :].rearrange("(p r) t -> p r t", r=4)
+            t0 = 0
+            for c, (width, share) in enumerate(chunks):
+                raw = keep.tile([P, 2, width], F32, name=f"raw{i}_{c}")
+                nc.sync.dma_start(raw[:], src[:, 2 * u : 2 * u + 2, t0 : t0 + width])
+                raws[i, c] = raw
+                t0 += width
+                if i == 0 and c == 0:
+                    nc.sync.dma_start(offsets[:], offs)
+                    for q in range(4):
+                        nc.scalar.dma_start(
+                            w_bytes[32 * q : 32 * q + 4, :, :].bitcast(I32),
+                            w_scales[:, 4 * q : 4 * q + 4, :].rearrange("a q m -> q a m").bitcast(I32),
+                        )
+
+        nc.gpsimd.dma_start(w_codes[:], w_words.rearrange("a p m r -> p a (m r)").bitcast(I32))
+        nc.gpsimd.dma_start(bias[:], b)
+
+        pairs = [keep.tile([P, T, 2], BF16, name=f"pairs{i}") for i in range(4)]
+        grouped = [keep.tile([P, S, 4], BF16, align_bytes=64, name=f"grouped{a}") for a in range(2)]
+        codes = [keep.tile([P, S], U32, align_bytes=64, name=f"codes{a}") for a in range(2)]
+        scales = [keep.tile([P, S], U8, align_bytes=64, name=f"scales{a}") for a in range(2)]
+        sums = [psum.tile([P, PIECE], F32, name=f"sums{s}") for s in range(S // PIECE)]
+
+        def cast(i):
+            t0 = 0
+            for c, (width, share) in enumerate(quarters[i][2]):
+                src = raws[i, c][:].rearrange("p e t -> p t e")
+                if share:
+                    nc.vector.tensor_copy(pairs[i][:, t0 : t0 + share, :], src[:, 0:share, :])
+                nc.scalar.activation(pairs[i][:, t0 + share : t0 + width, :], src[:, share:width, :], ACT.Copy)
+                t0 += width
+
+        def words(view):
+            return view.bitcast(U32)
+
+        def window(i, j0, j1):
+            return words(pairs[i][:].rearrange("p t e -> p (t e)")).indirect(offsets[:, j0 // 16 : j1 // 16])
+
+        def gather(i, j0, j1):
+            a, u, _ = quarters[i]
+            dst = words(grouped[a][:].rearrange("p j r -> p (j r)")).rearrange("p (j u) -> p j u", u=2)
+            nc.vector.tensor_copy(dst[:, j0:j1, u], window(i, j0, j1))
+
+        def quantise(a, j0, j1):
+            nc.vector.quantize_mx(
+                out=codes[a][:, j0:j1].bitcast(FP8X4),
+                scales=scales[a][:, j0:j1],
+                in_=grouped[a][:, j0:j1, :].rearrange("p j r -> p (j r)"),
+            )
+
+        def multiply(a, s):
+            cols = slice(s * PIECE, (s + 1) * PIECE)
+            nc.tensor.matmul_mx(
+                out=sums[s][:],
+                lhsT=w_codes[:, a, :].bitcast(FP8X4),
+                lhsT_scale=w_bytes[:, a, :],
+                rhs=codes[a][:, cols].bitcast(FP8X4),
+                rhs_scale=scales[a][:, cols],
+                start=(a == 0),
+                stop=(a == 1),
+            )
+
+        cast(0)
+        gather(0, 0, 512)
+        gather(0, 512, 1024)
+        cast(1)
+        gather(1, 0, 512)
+        gather(1, 512, 1024)
+        quantise(0, 0, 512)
+        cast(2)
+        gather(2, 0, 512)
+        gather(2, 512, 1024)
+        quantise(0, 512, 1024)
+        for s in range(4):
+            multiply(0, s)
+        cast(3)
+        plain = []
+        for s in range(3):
+            g = keep.tile([P, PIECE, 2], BF16, name=f"plain{s}")
+            nc.vector.tensor_copy(words(g[:].rearrange("p j e -> p (j e)")), window(3, s * PIECE, (s + 1) * PIECE))
+            nc.scalar.activation(grouped[1][:, s * PIECE : (s + 1) * PIECE, 2:4], g[:], ACT.Copy)
+        gather(3, 768, 1024)
+
+        results = [
+            keep.tile([P, 2 * PIECE], F32, name="result_ab"),
+            keep.tile([P, PIECE], F32, name="result_c"),
+            keep.tile([P, PIECE], F32, name="result_d"),
+        ]
+        place = [results[0][:, 0:PIECE], results[0][:, PIECE : 2 * PIECE], results[1][:], results[2][:]]
+        relus = [keep.tile([P, PIECE], F32, name=f"relu{s}") for s in range(4)]
+        for s in (0, 1, 3, 2):
+            quantise(1, s * PIECE, (s + 1) * PIECE)
+            multiply(1, s)
+        nc.scalar.activation(relus[0][:], sums[0][:], ACT.Relu, bias=bias[:])
+        nc.scalar.activation(place[0], relus[0][:], ACT.Square)
+        nc.scalar.activation(relus[1][:], sums[1][:], ACT.Relu, bias=bias[:])
+        nc.vector.tensor_tensor(place[1], relus[1][:], relus[1][:], ALU.mult)
+        nc.sync.dma_start(out[:, 0:512], results[0][:])
+        nc.vector.tensor_scalar(relus[3][:], sums[3][:], bias[:], 0.0, ALU.add, ALU.max)
+        nc.scalar.activation(place[3], relus[3][:], ACT.Square)
+        nc.sync.dma_start(out[:, 768:1024], results[2][:])
+        nc.vector.tensor_scalar(relus[2][:], sums[2][:], bias[:], 0.0, ALU.add, ALU.max)
+        nc.vector.tensor_tensor(place[2], relus[2][:], relus[2][:], ALU.mult)
+        nc.sync.dma_start(out[:, 512:768], results[1][:])

@@ -26,10 +26,10 @@ def tile_picked_pick_lin_relu2_sub_e_kernel(tc, xT, w_words, w_scales, b, offs, 
         psum = ctx.enter_context(tc.psum_pool(name="psum", bufs=1))
 
         quarters = [
-            (0, 0, [(1024, 640), (1024, 640)]),
-            (0, 1, [(1024, 256), (1024, 640)]),
-            (1, 0, [(1024, 0), (1024, 640)]),
-            (1, 1, [(768, 0), (768, 0), (512, 320)]),
+            (0, 0, [(1536, 896), (512, 256)]),
+            (0, 1, [(1536, 896), (512, 384)]),
+            (1, 0, [(1024, 0), (1024, 608)]),
+            (1, 1, [(896, 0), (896, 512), (256, 224)]),
         ]
 
         w_codes = keep.tile([P, 2, M], I32, align_bytes=64, name="w_codes")
@@ -59,9 +59,11 @@ def tile_picked_pick_lin_relu2_sub_e_kernel(tc, xT, w_words, w_scales, b, offs, 
 
         pairs = [keep.tile([P, T, 2], BF16, name=f"pairs{i}") for i in range(4)]
         grouped = [keep.tile([P, S, 4], BF16, align_bytes=64, name=f"grouped{a}") for a in range(2)]
+        picked = [keep.tile([P, 2, S, 2], BF16, align_bytes=64, name=f"picked{a}") for a in range(2)]
         codes = [keep.tile([P, S], U32, align_bytes=64, name=f"codes{a}") for a in range(2)]
         scales = [keep.tile([P, S], U8, align_bytes=64, name=f"scales{a}") for a in range(2)]
-        sums = [psum.tile([P, PIECE], F32, name=f"sums{s}") for s in range(S // PIECE)]
+        banks = [psum.tile([P, w], F32, name=f"sums{k}") for k, w in enumerate((512, 256, 256))]
+        sums = [banks[0][:, 0:256], banks[0][:, 256:512], banks[1][:], banks[2][:]]
 
         def cast(i):
             t0 = 0
@@ -80,8 +82,19 @@ def tile_picked_pick_lin_relu2_sub_e_kernel(tc, xT, w_words, w_scales, b, offs, 
 
         def gather(i, j0, j1):
             a, u, _ = quarters[i]
-            dst = words(grouped[a][:].rearrange("p j r -> p (j r)")).rearrange("p (j u) -> p j u", u=2)
-            nc.vector.tensor_copy(dst[:, j0:j1, u], window(i, j0, j1))
+            nc.vector.tensor_copy(words(picked[a][:, u, j0:j1, :].rearrange("p j e -> p (j e)")), window(i, j0, j1))
+
+        def interleave_vector(a, j0, j1):
+            nc.vector.tensor_copy(
+                grouped[a][:, j0:j1, :].rearrange("p j r -> p (j r)").bitcast(I32).rearrange("p (j u) -> p j u", u=2),
+                picked[a][:].rearrange("p u j e -> p (u j e)").bitcast(I32).rearrange("p (u j) -> p j u", u=2)[:, j0:j1, :],
+            )
+
+        def interleave_scalar(a, j0, j1):
+            nc.scalar.copy(
+                grouped[a][:, j0:j1, :].rearrange("p j r -> p (j r)").bitcast(F32).rearrange("p (j u) -> p j u", u=2),
+                picked[a][:].rearrange("p u j e -> p (u j e)").bitcast(F32).rearrange("p (u j) -> p j u", u=2)[:, j0:j1, :],
+            )
 
         def quantise(a, j0, j1):
             nc.vector.quantize_mx(
@@ -93,7 +106,7 @@ def tile_picked_pick_lin_relu2_sub_e_kernel(tc, xT, w_words, w_scales, b, offs, 
         def multiply(a, s):
             cols = slice(s * PIECE, (s + 1) * PIECE)
             nc.tensor.matmul_mx(
-                out=sums[s][:],
+                out=sums[s],
                 lhsT=w_codes[:, a, :].bitcast(FP8X4),
                 lhsT_scale=w_bytes[:, a, :],
                 rhs=codes[a][:, cols].bitcast(FP8X4),
@@ -108,39 +121,30 @@ def tile_picked_pick_lin_relu2_sub_e_kernel(tc, xT, w_words, w_scales, b, offs, 
         cast(1)
         gather(1, 0, 512)
         gather(1, 512, 1024)
+        interleave_vector(0, 0, 512)
+        interleave_vector(0, 512, 1024)
         quantise(0, 0, 512)
         cast(2)
         gather(2, 0, 512)
         gather(2, 512, 1024)
         quantise(0, 512, 1024)
-        for s in range(4):
-            multiply(0, s)
         cast(3)
-        plain = []
-        for s in range(3):
-            g = keep.tile([P, PIECE, 2], BF16, name=f"plain{s}")
-            nc.vector.tensor_copy(words(g[:].rearrange("p j e -> p (j e)")), window(3, s * PIECE, (s + 1) * PIECE))
-            nc.scalar.activation(grouped[1][:, s * PIECE : (s + 1) * PIECE, 2:4], g[:], ACT.Copy)
-        gather(3, 768, 1024)
+        for s in range(4):
+            gather(3, s * PIECE, (s + 1) * PIECE)
+            interleave_scalar(1, s * PIECE, (s + 1) * PIECE)
 
-        results = [
-            keep.tile([P, 2 * PIECE], F32, name="result_ab"),
-            keep.tile([P, PIECE], F32, name="result_c"),
-            keep.tile([P, PIECE], F32, name="result_d"),
-        ]
-        place = [results[0][:, 0:PIECE], results[0][:, PIECE : 2 * PIECE], results[1][:], results[2][:]]
-        relus = [keep.tile([P, PIECE], F32, name=f"relu{s}") for s in range(4)]
-        for s in (0, 1, 3, 2):
+        for s in range(4):
             quantise(1, s * PIECE, (s + 1) * PIECE)
+            multiply(0, s)
             multiply(1, s)
-        nc.scalar.activation(relus[0][:], sums[0][:], ACT.Relu, bias=bias[:])
-        nc.scalar.activation(place[0], relus[0][:], ACT.Square)
-        nc.scalar.activation(relus[1][:], sums[1][:], ACT.Relu, bias=bias[:])
-        nc.vector.tensor_tensor(place[1], relus[1][:], relus[1][:], ALU.mult)
-        nc.sync.dma_start(out[:, 0:512], results[0][:])
-        nc.vector.tensor_scalar(relus[3][:], sums[3][:], bias[:], 0.0, ALU.add, ALU.max)
-        nc.scalar.activation(place[3], relus[3][:], ACT.Square)
-        nc.sync.dma_start(out[:, 768:1024], results[2][:])
-        nc.vector.tensor_scalar(relus[2][:], sums[2][:], bias[:], 0.0, ALU.add, ALU.max)
-        nc.vector.tensor_tensor(place[2], relus[2][:], relus[2][:], ALU.mult)
+        relus = [keep.tile([P, w], F32, name=f"relu{k}") for k, w in enumerate((512, 256, 256))]
+        results = [keep.tile([P, w], F32, name=f"result{k}") for k, w in enumerate((512, 256, 256))]
+        nc.scalar.activation(relus[0][:], banks[0][:], ACT.Relu, bias=bias[:])
+        nc.vector.tensor_scalar(relus[1][:], banks[1][:], bias[:], 0.0, ALU.add, ALU.max)
+        nc.vector.tensor_tensor(results[1][:], relus[1][:], relus[1][:], ALU.mult)
+        nc.scalar.activation(relus[2][:], banks[2][:], ACT.Relu, bias=bias[:])
+        nc.scalar.activation(results[0][:], relus[0][:], ACT.Square)
+        nc.vector.tensor_tensor(results[2][:], relus[2][:], relus[2][:], ALU.mult)
         nc.sync.dma_start(out[:, 512:768], results[1][:])
+        nc.sync.dma_start(out[:, 0:512], results[0][:])
+        nc.sync.dma_start(out[:, 768:1024], results[2][:])

@@ -26,10 +26,10 @@ def tile_picked_pick_lin_relu2_sub_e_kernel(tc, xT, w_words, w_scales, b, offs, 
         psum = ctx.enter_context(tc.psum_pool(name="psum", bufs=1))
 
         quarters = [
-            (0, 0, [(1536, 896), (512, 256)]),
-            (0, 1, [(1536, 896), (512, 384)]),
-            (1, 0, [(1024, 0), (1024, 608)]),
-            (1, 1, [(896, 0), (896, 512), (256, 224)]),
+            (0, 0, [(2048, 1376)]),
+            (0, 1, [(2048, 1376)]),
+            (1, 0, [(1024, 0), (1024, 128)]),
+            (1, 1, [(896, 0), (896, 352), (256, 256)]),
         ]
 
         w_codes = keep.tile([P, 2, M], I32, align_bytes=64, name="w_codes")
@@ -62,8 +62,8 @@ def tile_picked_pick_lin_relu2_sub_e_kernel(tc, xT, w_words, w_scales, b, offs, 
         picked = [keep.tile([P, 2, S, 2], BF16, align_bytes=64, name=f"picked{a}") for a in range(2)]
         codes = [keep.tile([P, S], U32, align_bytes=64, name=f"codes{a}") for a in range(2)]
         scales = [keep.tile([P, S], U8, align_bytes=64, name=f"scales{a}") for a in range(2)]
-        banks = [psum.tile([P, w], F32, name=f"sums{k}") for k, w in enumerate((512, 256, 256))]
-        sums = [banks[0][:, 0:256], banks[0][:, 256:512], banks[1][:], banks[2][:]]
+        spans = [(0, 256), (256, 512), (512, 768), (768, 896), (896, 1024)]
+        sums = [psum.tile([P, j1 - j0], F32, name=f"sums{k}") for k, (j0, j1) in enumerate(spans)]
 
         def cast(i):
             t0 = 0
@@ -71,7 +71,8 @@ def tile_picked_pick_lin_relu2_sub_e_kernel(tc, xT, w_words, w_scales, b, offs, 
                 src = raws[i, c][:].rearrange("p e t -> p t e")
                 if share:
                     nc.vector.tensor_copy(pairs[i][:, t0 : t0 + share, :], src[:, 0:share, :])
-                nc.scalar.activation(pairs[i][:, t0 + share : t0 + width, :], src[:, share:width, :], ACT.Copy)
+                if share < width:
+                    nc.scalar.activation(pairs[i][:, t0 + share : t0 + width, :], src[:, share:width, :], ACT.Copy)
                 t0 += width
 
         def words(view):
@@ -103,10 +104,10 @@ def tile_picked_pick_lin_relu2_sub_e_kernel(tc, xT, w_words, w_scales, b, offs, 
                 in_=grouped[a][:, j0:j1, :].rearrange("p j r -> p (j r)"),
             )
 
-        def multiply(a, s):
-            cols = slice(s * PIECE, (s + 1) * PIECE)
+        def multiply(a, k):
+            cols = slice(*spans[k])
             nc.tensor.matmul_mx(
-                out=sums[s],
+                out=sums[k][:],
                 lhsT=w_codes[:, a, :].bitcast(FP8X4),
                 lhsT_scale=w_bytes[:, a, :],
                 rhs=codes[a][:, cols].bitcast(FP8X4),
@@ -116,18 +117,13 @@ def tile_picked_pick_lin_relu2_sub_e_kernel(tc, xT, w_words, w_scales, b, offs, 
             )
 
         cast(0)
-        gather(0, 0, 512)
-        gather(0, 512, 1024)
+        gather(0, 0, S)
         cast(1)
-        gather(1, 0, 512)
-        gather(1, 512, 1024)
-        interleave_vector(0, 0, 512)
-        interleave_vector(0, 512, 1024)
-        quantise(0, 0, 512)
+        gather(1, 0, S)
+        interleave_vector(0, 0, S)
+        quantise(0, 0, S)
         cast(2)
-        gather(2, 0, 512)
-        gather(2, 512, 1024)
-        quantise(0, 512, 1024)
+        gather(2, 0, S)
         cast(3)
         for s in range(4):
             gather(3, s * PIECE, (s + 1) * PIECE)
@@ -135,16 +131,28 @@ def tile_picked_pick_lin_relu2_sub_e_kernel(tc, xT, w_words, w_scales, b, offs, 
 
         for s in range(4):
             quantise(1, s * PIECE, (s + 1) * PIECE)
-            multiply(0, s)
-            multiply(1, s)
-        relus = [keep.tile([P, w], F32, name=f"relu{k}") for k, w in enumerate((512, 256, 256))]
+            for k in ((3, 4) if s == 3 else (s,)):
+                multiply(0, k)
+                multiply(1, k)
+
+        relus = keep.tile([P, S], F32, name="relus")
         results = [keep.tile([P, w], F32, name=f"result{k}") for k, w in enumerate((512, 256, 256))]
-        nc.scalar.activation(relus[0][:], banks[0][:], ACT.Relu, bias=bias[:])
-        nc.vector.tensor_scalar(relus[1][:], banks[1][:], bias[:], 0.0, ALU.add, ALU.max)
-        nc.vector.tensor_tensor(results[1][:], relus[1][:], relus[1][:], ALU.mult)
-        nc.scalar.activation(relus[2][:], banks[2][:], ACT.Relu, bias=bias[:])
-        nc.scalar.activation(results[0][:], relus[0][:], ACT.Square)
-        nc.vector.tensor_tensor(results[2][:], relus[2][:], relus[2][:], ALU.mult)
-        nc.sync.dma_start(out[:, 512:768], results[1][:])
+
+        def finish_scalar(k, dst):
+            j0, j1 = spans[k]
+            nc.scalar.activation(relus[:, j0:j1], sums[k][:], ACT.Relu, bias=bias[:])
+            nc.scalar.activation(dst, relus[:, j0:j1], ACT.Square)
+
+        def finish_vector(k, dst):
+            j0, j1 = spans[k]
+            nc.vector.tensor_scalar(relus[:, j0:j1], sums[k][:], bias[:], 0.0, ALU.add, ALU.max)
+            nc.vector.tensor_tensor(dst, relus[:, j0:j1], relus[:, j0:j1], ALU.mult)
+
+        finish_scalar(0, results[0][:, 0:256])
+        finish_scalar(1, results[0][:, 256:512])
         nc.sync.dma_start(out[:, 0:512], results[0][:])
+        finish_vector(2, results[1][:])
+        nc.sync.dma_start(out[:, 512:768], results[1][:])
+        finish_vector(3, results[2][:, 0:128])
+        finish_scalar(4, results[2][:, 128:256])
         nc.sync.dma_start(out[:, 768:1024], results[2][:])

@@ -54,7 +54,7 @@ def tile_picked_pick_lin_relu2_sub_e_kernel(tc, xT, w_words, w_scales, b, offs, 
                             w_scales[:, 4 * q : 4 * q + 4, :].rearrange("a q m -> q a m").bitcast(I32),
                         )
 
-        nc.gpsimd.dma_start(w_codes[:], w_words.rearrange("a p m r -> p a (m r)").bitcast(I32))
+        nc.sync.dma_start(w_codes[:], w_words.rearrange("a p m r -> p a (m r)").bitcast(I32))
         nc.gpsimd.dma_start(bias[:], b)
 
         pairs = [keep.tile([P, T, 2], BF16, name=f"pairs{i}") for i in range(4)]

from contextlib import ExitStack

import concourse.mybir as mybir

K, T, S, M = 1024, 2048, 1024, 128
P = 128
FLOPS = 2 * K * S * M

F32 = mybir.dt.float32
BF16 = mybir.dt.bfloat16
I32 = mybir.dt.int32
U32 = mybir.dt.uint32
U16 = mybir.dt.uint16
U8 = mybir.dt.uint8
FP8X4 = mybir.dt.float8_e4m3fn_x4
ACT = mybir.ActivationFunctionType
ALU = mybir.AluOpType

PIECE = 256


def tile_picked_pick_lin_relu2_sub_e_kernel(tc, xT, w_words, w_scales, b, offs, out):
    nc = tc.nc
    with ExitStack() as ctx:
        keep = ctx.enter_context(tc.tile_pool(name="keep", bufs=1))
        psum = ctx.enter_context(tc.psum_pool(name="psum", bufs=1))

        quarters = [
            (0, 0, [(2048, 1376)]),
            (0, 1, [(2048, 1376)]),
            (1, 0, [(1024, 0), (1024, 128)]),
            (1, 1, [(896, 0), (896, 352), (256, 256)]),
        ]

        w_codes = keep.tile([P, 2, M], I32, align_bytes=64, name="w_codes")
        w_bytes = keep.tile([P, 2, M], U8, align_bytes=64, name="w_bytes")
        bias = keep.tile([P, 1], F32, name="bias")
        nc.gpsimd.memset(w_bytes[:], 0)
        offsets = keep.tile([P, S // 16], U16, name="offsets")
        raws = {}
        for i, (a, u, chunks) in enumerate(quarters):
            src = xT[512 * a : 512 * (a + 1), :].rearrange("(p r) t -> p r t", r=4)
            t0 = 0
            for c, (width, share) in enumerate(chunks):
                raw = keep.tile([P, 2, width], F32, name=f"raw{i}_{c}")
                nc.sync.dma_start(raw[:], src[:, 2 * u : 2 * u + 2, t0 : t0 + width])
                raws[i, c] = raw
                t0 += width
                if i == 0 and c == 0:
                    nc.sync.dma_start(offsets[:], offs)
                    for q in range(4):
                        nc.scalar.dma_start(
                            w_bytes[32 * q : 32 * q + 4, :, :].bitcast(I32),
                            w_scales[:, 4 * q : 4 * q + 4, :].rearrange("a q m -> q a m").bitcast(I32),
                        )

        nc.sync.dma_start(w_codes[:], w_words.rearrange("a p m r -> p a (m r)").bitcast(I32))
        nc.gpsimd.dma_start(bias[:], b)

        pairs = [keep.tile([P, T, 2], BF16, name=f"pairs{i}") for i in range(4)]
        grouped = [keep.tile([P, S, 4], BF16, align_bytes=64, name=f"grouped{a}") for a in range(2)]
        picked = [keep.tile([P, 2, S, 2], BF16, align_bytes=64, name=f"picked{a}") for a in range(2)]
        codes = [keep.tile([P, S], U32, align_bytes=64, name=f"codes{a}") for a in range(2)]
        scales = [keep.tile([P, S], U8, align_bytes=64, name=f"scales{a}") for a in range(2)]
        spans = [(0, 256), (256, 512), (512, 768), (768, 896), (896, 1024)]
        sums = [psum.tile([P, j1 - j0], F32, name=f"sums{k}") for k, (j0, j1) in enumerate(spans)]

        def cast(i):
            t0 = 0
            for c, (width, share) in enumerate(quarters[i][2]):
                src = raws[i, c][:].rearrange("p e t -> p t e")
                if share:
                    nc.vector.tensor_copy(pairs[i][:, t0 : t0 + share, :], src[:, 0:share, :])
                if share < width:
                    nc.scalar.activation(pairs[i][:, t0 + share : t0 + width, :], src[:, share:width, :], ACT.Copy)
                t0 += width

        def words(view):
            return view.bitcast(U32)

        def window(i, j0, j1):
            return words(pairs[i][:].rearrange("p t e -> p (t e)")).indirect(offsets[:, j0 // 16 : j1 // 16])

        def gather(i, j0, j1):
            a, u, _ = quarters[i]
            nc.vector.tensor_copy(words(picked[a][:, u, j0:j1, :].rearrange("p j e -> p (j e)")), window(i, j0, j1))

        def interleave_vector(a, j0, j1):
            nc.vector.tensor_copy(
                grouped[a][:, j0:j1, :].rearrange("p j r -> p (j r)").bitcast(I32).rearrange("p (j u) -> p j u", u=2),
                picked[a][:].rearrange("p u j e -> p (u j e)").bitcast(I32).rearrange("p (u j) -> p j u", u=2)[:, j0:j1, :],
            )

        def interleave_scalar(a, j0, j1):
            nc.scalar.copy(
                grouped[a][:, j0:j1, :].rearrange("p j r -> p (j r)").bitcast(F32).rearrange("p (j u) -> p j u", u=2),
                picked[a][:].rearrange("p u j e -> p (u j e)").bitcast(F32).rearrange("p (u j) -> p j u", u=2)[:, j0:j1, :],
            )

        def quantise(a, j0, j1):
            nc.vector.quantize_mx(
                out=codes[a][:, j0:j1].bitcast(FP8X4),
                scales=scales[a][:, j0:j1],
                in_=grouped[a][:, j0:j1, :].rearrange("p j r -> p (j r)"),
            )

        def multiply(a, k):
            cols = slice(*spans[k])
            nc.tensor.matmul_mx(
                out=sums[k][:],
                lhsT=w_codes[:, a, :].bitcast(FP8X4),
                lhsT_scale=w_bytes[:, a, :],
                rhs=codes[a][:, cols].bitcast(FP8X4),
                rhs_scale=scales[a][:, cols],
                start=(a == 0),
                stop=(a == 1),
            )

        cast(0)
        gather(0, 0, S)
        cast(1)
        gather(1, 0, S)
        interleave_vector(0, 0, S)
        quantise(0, 0, S)
        cast(2)
        gather(2, 0, S)
        cast(3)
        for s in range(4):
            gather(3, s * PIECE, (s + 1) * PIECE)
            interleave_scalar(1, s * PIECE, (s + 1) * PIECE)

        for s in range(4):
            quantise(1, s * PIECE, (s + 1) * PIECE)
            for k in ((3, 4) if s == 3 else (s,)):
                multiply(0, k)
                multiply(1, k)

        relus = keep.tile([P, S], F32, name="relus")
        results = [keep.tile([P, w], F32, name=f"result{k}") for k, w in enumerate((512, 256, 256))]

        def finish_scalar(k, dst):
            j0, j1 = spans[k]
            nc.scalar.activation(relus[:, j0:j1], sums[k][:], ACT.Relu, bias=bias[:])
            nc.scalar.activation(dst, relus[:, j0:j1], ACT.Square)

        def finish_vector(k, dst):
            j0, j1 = spans[k]
            nc.vector.tensor_scalar(relus[:, j0:j1], sums[k][:], bias[:], 0.0, ALU.add, ALU.max)
            nc.vector.tensor_tensor(dst, relus[:, j0:j1], relus[:, j0:j1], ALU.mult)

        finish_scalar(0, results[0][:, 0:256])
        finish_scalar(1, results[0][:, 256:512])
        nc.sync.dma_start(out[:, 0:512], results[0][:])
        finish_vector(2, results[1][:])
        nc.sync.dma_start(out[:, 512:768], results[1][:])
        finish_vector(3, results[2][:, 0:128])
        finish_scalar(4, results[2][:, 128:256])
        nc.sync.dma_start(out[:, 768:1024], results[2][:])
